import numpy as np
import ml_dtypes


def mxq(x, axis, fmt="e4m3"):
    dtype, down = {"e4m3": (ml_dtypes.float8_e4m3fn, 7), "e5m2": (ml_dtypes.float8_e5m2, 14)}[fmt]
    v = np.moveaxis(np.asarray(x, np.float32).astype(ml_dtypes.bfloat16).astype(np.float64), axis, -1)
    blocks = v.reshape(v.shape[:-1] + (-1, 32))
    amax = np.abs(blocks).max(-1, keepdims=True)
    byte = np.maximum(np.where(amax > 0, np.frexp(amax)[1] - 1 + 127, 0) - down, 1)
    scale = np.exp2(byte - 127.0)
    codes = (blocks / scale).astype(np.float32).astype(dtype).astype(np.float64)
    return np.moveaxis((codes * scale).reshape(v.shape), -1, axis)


WIDE = False


def mx_kscale(k):
    if not WIDE:
        return np.ones(k)
    levels = np.array([10, -10, 5, -5, 0])
    if k % 512:
        return np.exp2(np.random.permutation(np.resize(levels, k // 32))).repeat(32)
    a = np.empty((k // 512, 16))
    for p in range(k // 512):
        a[p, :8] = np.random.permutation(np.resize(levels, 8))
        for g in range(8):
            far = levels[np.abs(levels - a[p, g]) >= 10]
            a[p, g + 8] = far[np.random.randint(len(far))]
    return np.exp2(a.ravel()).repeat(32)


def f64(x):
    return np.asarray(x).astype(np.float64)


def striped(idx):
    return np.tile(idx.reshape(-1, 16).T, (8, 1)).astype(np.uint16)


def unstriped(offs):
    return offs[:16].T.reshape(-1).astype(np.int64)


def pack_weight(w):
    k, n = w.shape
    w = f64(np.asarray(w, np.float32).astype(ml_dtypes.bfloat16)).reshape(k // 32, 32, n)
    amax = np.abs(w).max(1)
    byte = np.clip(np.where(amax > 0, np.frexp(amax)[1] - 1 + 127 - 7, 1), 1, 254)
    scaled = (w * np.exp2(127.0 - byte)[:, None, :]).reshape(k, n).astype(np.float32)
    words = np.ascontiguousarray(scaled.reshape(k // 512, 128, 4, n).transpose(0, 1, 3, 2)).astype(ml_dtypes.float8_e4m3fn).view(np.uint8)
    return words, np.ascontiguousarray(byte.astype(np.uint8).reshape(k // 512, 16, n))


def unpack_weight(words, scales):
    g, p, n, _ = words.shape
    vals = np.ascontiguousarray(words).view(ml_dtypes.float8_e4m3fn).astype(np.float64) * np.repeat(np.exp2(scales.astype(np.float64) - 127.0), 8, axis=1)[..., None]
    return vals.transpose(0, 1, 3, 2).reshape(g * 512, n)


K, T, D, S, V, N = 1024, 512, 4, 1024, 256, 512


def setup_inputs():
    n = np.random.standard_normal
    s = mx_kscale(K)[:, None]
    words, scales = pack_weight(n((K, N)) / np.sqrt(K) / s)
    return {
        "xT": (n((K, T)) * s).astype(np.float32),
        "w_words": words,
        "w_scales": scales,
        "b": (0.3 * n((N, 1))).astype(np.float32),
        "gate": np.tile(np.random.uniform(0.2, 1.0, (D, 1, V)) / np.sqrt(D), (1, N, 1)).astype(np.float32),
        "pos1": striped(np.random.permutation(T)[:V]),
        "pos2": striped(np.random.permutation(T)[:V]),
        "pos3": striped(np.random.permutation(T)[:V]),
        "pos4": striped(np.random.permutation(T)[:V]),
    }


def reference(xT, w_words, w_scales, b, gate, pos1, pos2, pos3, pos4):
    w = unpack_weight(w_words, w_scales)
    y = w.T @ mxq(f64(xT), 0, "e4m3")
    y = y + f64(b)
    return sum(f64(gate[d]) * y[:, unstriped(p)] for d, p in enumerate((pos1, pos2, pos3, pos4)))

@@ -1,0 +1,184 @@
+from contextlib import ExitStack
+
+import concourse.mybir as mybir
+
+K, T, D, V, N = 1024, 512, 4, 256, 512
+
+F32 = mybir.dt.float32
+BF16 = mybir.dt.bfloat16
+U32 = mybir.dt.uint32
+I32 = mybir.dt.int32
+U16 = mybir.dt.uint16
+U8 = mybir.dt.uint8
+FP8X4 = mybir.dt.float8_e4m3fn_x4
+ADD = mybir.AluOpType.add
+MULT = mybir.AluOpType.mult
+IDENTITY = mybir.ActivationFunctionType.Identity
+
+FLOPS = 2 * K * T * N + 2 * D * N * V
+
+P = 128
+PACK = 4
+K_PASS = P * PACK
+PASSES = K // K_PASS
+BLOCKS = N // P
+HALF = T // 2
+SPLIT = 336
+
+
+def interleave(nc, grouped, raw, lanes, c0, c1, scalar):
+    out = grouped[:, c0:c1, lanes]
+    in_ = raw[:, lanes, c0:c1].rearrange("p j t -> p t j")
+    if scalar:
+        nc.scalar.copy(out=out, in_=in_)
+    else:
+        nc.vector.tensor_copy(out=out, in_=in_)
+
+
+def tile_picked_agg_lin_bias_sub_l_kernel(tc, xT, w_words, w_scales, b, gate, pos1, pos2, pos3, pos4, out):
+    nc = tc.nc
+    with ExitStack() as ctx:
+        keep = ctx.enter_context(tc.tile_pool(name="keep", bufs=1))
+        ypool = ctx.enter_context(tc.tile_pool(name="ypool", bufs=2))
+        work = ctx.enter_context(tc.tile_pool(name="work", bufs=2))
+        psum = ctx.enter_context(tc.psum_pool(name="psum", bufs=1))
+
+        lists = [keep.tile([P, V // 16], U16, name=f"list{d}") for d in range(D)]
+        warm = keep.tile([P, 1], F32, name="warm")
+        warm_out = keep.tile([P, 1], F32, name="warm_out")
+        bias = keep.tile([P, BLOCKS], F32, name="bias")
+        w_planes = keep.tile([P, N], U8, name="w_planes", align_bytes=256)
+        w_codes = keep.tile([P, PASSES, N], U32, name="w_codes", align_bytes=256)
+        raw = [keep.tile([P, PACK, T], F32, name=f"raw{a}", align_bytes=256) for a in range(PASSES)]
+        grouped = [keep.tile([P, T, PACK], BF16, name=f"grouped{a}", align_bytes=256) for a in range(PASSES)]
+        x_codes = [keep.tile([P, T], U32, name=f"x_codes{a}", align_bytes=256) for a in range(PASSES)]
+        x_planes = [keep.tile([P, T], U8, name=f"x_planes{a}", align_bytes=256) for a in range(PASSES)]
+        gates = [keep.tile([P, D, V], F32, name=f"gates{c}", align_bytes=256) for c in range(BLOCKS)]
+
+        nc.vector.memset(w_planes[:].bitcast(I32), 0)
+        nc.vector.memset(warm[:], 0.0)
+        nc.scalar.activation(out=warm_out[:], in_=warm[:], func=IDENTITY)
+
+        for q in range(4):
+            nc.scalar.dma_start(
+                out=w_planes[32 * q : 32 * q + 4 * PASSES, :].bitcast(I32),
+                in_=w_scales[:, 4 * q : 4 * q + 4, :].bitcast(I32),
+            )
+
+        w_view = w_words.rearrange("a p m r -> p a (m r)")
+
+        def load_weights(m0, m1):
+            nc.sync.dma_start(
+                out=w_codes[:, :, m0:m1].bitcast(I32),
+                in_=w_view[:, :, PACK * m0 : PACK * m1].bitcast(I32),
+            )
+
+        def load_x(a, lanes):
+            nc.sync.dma_start(
+                out=raw[a][:, lanes, :],
+                in_=xT[a * K_PASS : (a + 1) * K_PASS, :].rearrange("(p j) t -> p j t", j=PACK)[:, lanes, :],
+            )
+
+        load_weights(0, P)
+        load_x(0, slice(0, PACK))
+        load_x(1, slice(0, 2))
+        load_x(1, slice(2, PACK))
+        nc.sync.dma_start(out=bias[:], in_=b.rearrange("(c p) o -> p (c o)", p=P))
+        for d, pos in enumerate((pos1, pos2, pos3, pos4)):
+            nc.sync.dma_start(out=lists[d][:], in_=pos)
+            nc.sync.dma_start(out=gates[0][:, d, :], in_=gate[d, 0:P, :])
+        load_weights(P, N)
+        for c in range(1, BLOCKS):
+            nc.sync.dma_start(out=gates[c][:], in_=gate[:, c * P : (c + 1) * P, :].rearrange("d p v -> p d v"))
+
+        def quantize(a, c0, c1):
+            nc.vector.quantize_mx(
+                out=x_codes[a][:, c0:c1].bitcast(FP8X4),
+                scales=x_planes[a][:, c0:c1],
+                in_=grouped[a][:, c0:c1, :].rearrange("p t j -> p (t j)"),
+            )
+
+        everything = slice(0, PACK)
+        interleave(nc, grouped[0], raw[0], everything, 0, HALF, False)
+        interleave(nc, grouped[0], raw[0], everything, SPLIT, T, True)
+        interleave(nc, grouped[0], raw[0], everything, HALF, SPLIT, False)
+        quantize(0, 0, T)
+        for lanes in (slice(0, 2), slice(2, PACK)):
+            interleave(nc, grouped[1], raw[1], lanes, 0, HALF, False)
+            interleave(nc, grouped[1], raw[1], lanes, SPLIT, T, True)
+            interleave(nc, grouped[1], raw[1], lanes, HALF, SPLIT, False)
+        quantize(1, 0, HALF)
+        quantize(1, HALF, T)
+
+        def project(c):
+            y = ypool.tile([P, T], F32, name="y")
+            cols = slice(c * P, (c + 1) * P)
+            accs = [psum.tile([P, HALF], F32, name=f"acc{h}") for h in range(2)]
+            for a in range(PASSES):
+                for h in range(2):
+                    t_cols = slice(h * HALF, (h + 1) * HALF)
+                    nc.tensor.matmul_mx(
+                        out=accs[h][:],
+                        lhsT=w_codes[:, a, cols].bitcast(FP8X4),
+                        lhsT_scale=w_planes[4 * a : P, cols],
+                        rhs=x_codes[a][:, t_cols].bitcast(FP8X4),
+                        rhs_scale=x_planes[a][:, t_cols],
+                        start=(a == 0),
+                        stop=(a == PASSES - 1),
+                    )
+            for h in range(2):
+                nc.scalar.activation(
+                    out=y[:, h * HALF : (h + 1) * HALF], in_=accs[h][:], func=IDENTITY, bias=bias[:, c : c + 1]
+                )
+            return y
+
+        def gather(y, products, c, d, v0, v1):
+            nc.vector.tensor_tensor(
+                out=products[:, d, v0:v1],
+                in0=y[:].indirect(lists[d][:, v0 // 16 : v1 // 16]),
+                in1=gates[c][:, d, v0:v1],
+                op=MULT,
+            )
+
+        def new_tiles():
+            products = work.tile([P, D, V], F32, name="products", align_bytes=64)
+            pairs = work.tile([P, 2, V], F32, name="pairs", align_bytes=64)
+            sums = work.tile([P, V], F32, name="sums", align_bytes=64)
+            return products, pairs, sums
+
+        def add_pairs(tiles):
+            products, pairs, sums = tiles
+            nc.vector.tensor_tensor(out=pairs[:], in0=products[:, 0:2, :], in1=products[:, 2:4, :], op=ADD)
+
+        def add_rest(tiles, c):
+            products, pairs, sums = tiles
+            nc.vector.tensor_tensor(out=sums[:], in0=pairs[:, 0, :], in1=pairs[:, 1, :], op=ADD)
+            nc.sync.dma_start(out=out[c * P : (c + 1) * P, :], in_=sums[:])
+
+        ys = [project(0)]
+        before = None
+        for c in range(BLOCKS - 1):
+            ys.append(project(c + 1))
+            tiles = new_tiles()
+            gather(ys[c], tiles[0], c, 0, 0, V)
+            if before is not None:
+                add_pairs(before)
+            gather(ys[c], tiles[0], c, 1, 0, V)
+            if before is not None:
+                add_rest(before, c - 1)
+            gather(ys[c], tiles[0], c, 2, 0, V)
+            gather(ys[c], tiles[0], c, 3, 0, V)
+            before = tiles
+
+        c = BLOCKS - 1
+        products, pairs, sums = new_tiles()
+        gather(ys[c], products, c, 0, 0, V)
+        add_pairs(before)
+        gather(ys[c], products, c, 1, 0, V)
+        add_rest(before, c - 1)
+        gather(ys[c], products, c, 2, 0, V)
+        nc.vector.tensor_tensor(out=pairs[:, 0, :], in0=products[:, 0, :], in1=products[:, 1, :], op=ADD)
+        gather(ys[c], products, c, 3, 0, V)
+        nc.vector.tensor_tensor(out=pairs[:, 1, :], in0=pairs[:, 0, :], in1=products[:, 2, :], op=ADD)
+        nc.vector.tensor_tensor(out=sums[:], in0=pairs[:, 1, :], in1=products[:, 3, :], op=ADD)
+        nc.sync.dma_start(out=out[c * P : N, :], in_=sums[:])

@@ -22,7 +22,7 @@ PACK = 4
 K_PASS = P * PACK
 PASSES = K // K_PASS
 BLOCKS = N // P
-HALF = T // 2
+PIECES = ((0, 256), (256, 384), (384, 512))
 SPLIT = 336
 
 
@@ -39,8 +39,7 @@ def tile_picked_agg_lin_bias_sub_l_kernel(tc, xT, w_words, w_scales, b, gate, po
     nc = tc.nc
     with ExitStack() as ctx:
         keep = ctx.enter_context(tc.tile_pool(name="keep", bufs=1))
-        ypool = ctx.enter_context(tc.tile_pool(name="ypool", bufs=2))
-        work = ctx.enter_context(tc.tile_pool(name="work", bufs=2))
+        ypool = ctx.enter_context(tc.tile_pool(name="ypool", bufs=3))
         psum = ctx.enter_context(tc.psum_pool(name="psum", bufs=1))
 
         lists = [keep.tile([P, V // 16], U16, name=f"list{d}") for d in range(D)]
@@ -55,22 +54,12 @@ def tile_picked_agg_lin_bias_sub_l_kernel(tc, xT, w_words, w_scales, b, gate, po
         x_planes = [keep.tile([P, T], U8, name=f"x_planes{a}", align_bytes=256) for a in range(PASSES)]
         gates = [keep.tile([P, D, V], F32, name=f"gates{c}", align_bytes=256) for c in range(BLOCKS)]
 
-        nc.vector.memset(w_planes[:].bitcast(I32), 0)
-        nc.vector.memset(warm[:], 0.0)
-        nc.scalar.activation(out=warm_out[:], in_=warm[:], func=IDENTITY)
-
-        for q in range(4):
-            nc.scalar.dma_start(
-                out=w_planes[32 * q : 32 * q + 4 * PASSES, :].bitcast(I32),
-                in_=w_scales[:, 4 * q : 4 * q + 4, :].bitcast(I32),
-            )
-
         w_view = w_words.rearrange("a p m r -> p a (m r)")
 
-        def load_weights(m0, m1):
+        def load_weights(a0, a1, m0, m1):
             nc.sync.dma_start(
-                out=w_codes[:, :, m0:m1].bitcast(I32),
-                in_=w_view[:, :, PACK * m0 : PACK * m1].bitcast(I32),
+                out=w_codes[:, a0:a1, m0:m1].bitcast(I32),
+                in_=w_view[:, a0:a1, PACK * m0 : PACK * m1].bitcast(I32),
             )
 
         def load_x(a, lanes):
@@ -79,17 +68,38 @@ def tile_picked_agg_lin_bias_sub_l_kernel(tc, xT, w_words, w_scales, b, gate, po
                 in_=xT[a * K_PASS : (a + 1) * K_PASS, :].rearrange("(p j) t -> p j t", j=PACK)[:, lanes, :],
             )
 
-        load_weights(0, P)
+        def load_gates(c, d0, d1):
+            nc.sync.dma_start(
+                out=gates[c][:, d0:d1, :],
+                in_=gate[d0:d1, c * P : (c + 1) * P, :].rearrange("d p v -> p d v"),
+            )
+
+        nc.vector.memset(w_planes[:].bitcast(I32), 0)
+        nc.vector.memset(warm[:], 0.0)
+        nc.scalar.activation(out=warm_out[:], in_=warm[:], func=IDENTITY)
         load_x(0, slice(0, PACK))
+        for q in range(4):
+            nc.sync.dma_start(
+                out=w_planes[32 * q : 32 * q + 4 * PASSES, :].bitcast(I32),
+                in_=w_scales[:, 4 * q : 4 * q + 4, :].bitcast(I32),
+            )
         load_x(1, slice(0, 2))
+        load_weights(0, 1, 0, P)
         load_x(1, slice(2, PACK))
+        load_weights(1, 2, 0, P)
         nc.sync.dma_start(out=bias[:], in_=b.rearrange("(c p) o -> p (c o)", p=P))
-        for d, pos in enumerate((pos1, pos2, pos3, pos4)):
-            nc.sync.dma_start(out=lists[d][:], in_=pos)
-            nc.sync.dma_start(out=gates[0][:, d, :], in_=gate[d, 0:P, :])
-        load_weights(P, N)
-        for c in range(1, BLOCKS):
-            nc.sync.dma_start(out=gates[c][:], in_=gate[:, c * P : (c + 1) * P, :].rearrange("d p v -> p d v"))
+        nc.sync.dma_start(out=lists[0][:], in_=pos1)
+        load_gates(0, 0, 2)
+        nc.sync.dma_start(out=lists[1][:], in_=pos2)
+        nc.sync.dma_start(out=lists[2][:], in_=pos3)
+        nc.sync.dma_start(out=lists[3][:], in_=pos4)
+        load_gates(0, 2, D)
+        load_weights(0, PASSES, P, 2 * P)
+        load_gates(1, 0, D)
+        load_weights(0, PASSES, 2 * P, N)
+        load_gates(2, 0, D)
+        load_gates(3, 0, D)
+
 
         def quantize(a, c0, c1):
             nc.vector.quantize_mx(
@@ -98,87 +108,77 @@ def tile_picked_agg_lin_bias_sub_l_kernel(tc, xT, w_words, w_scales, b, gate, po
                 in_=grouped[a][:, c0:c1, :].rearrange("p t j -> p (t j)"),
             )
 
+        first = PIECES[0][1]
         everything = slice(0, PACK)
-        interleave(nc, grouped[0], raw[0], everything, 0, HALF, False)
+        interleave(nc, grouped[0], raw[0], everything, 0, first, False)
         interleave(nc, grouped[0], raw[0], everything, SPLIT, T, True)
-        interleave(nc, grouped[0], raw[0], everything, HALF, SPLIT, False)
+        interleave(nc, grouped[0], raw[0], everything, first, SPLIT, False)
         quantize(0, 0, T)
         for lanes in (slice(0, 2), slice(2, PACK)):
-            interleave(nc, grouped[1], raw[1], lanes, 0, HALF, False)
+            interleave(nc, grouped[1], raw[1], lanes, 0, first, False)
             interleave(nc, grouped[1], raw[1], lanes, SPLIT, T, True)
-            interleave(nc, grouped[1], raw[1], lanes, HALF, SPLIT, False)
-        quantize(1, 0, HALF)
-        quantize(1, HALF, T)
+            interleave(nc, grouped[1], raw[1], lanes, first, SPLIT, False)
+        for t0, t1 in PIECES:
+            quantize(1, t0, t1)
 
         def project(c):
             y = ypool.tile([P, T], F32, name="y")
             cols = slice(c * P, (c + 1) * P)
-            accs = [psum.tile([P, HALF], F32, name=f"acc{h}") for h in range(2)]
+            accs = [psum.tile([P, t1 - t0], F32, name=f"acc{t0}") for t0, t1 in PIECES]
             for a in range(PASSES):
-                for h in range(2):
-                    t_cols = slice(h * HALF, (h + 1) * HALF)
+                for acc, (t0, t1) in zip(accs, PIECES):
                     nc.tensor.matmul_mx(
-                        out=accs[h][:],
+                        out=acc[:],
                         lhsT=w_codes[:, a, cols].bitcast(FP8X4),
                         lhsT_scale=w_planes[4 * a : P, cols],
-                        rhs=x_codes[a][:, t_cols].bitcast(FP8X4),
-                        rhs_scale=x_planes[a][:, t_cols],
+                        rhs=x_codes[a][:, t0:t1].bitcast(FP8X4),
+                        rhs_scale=x_planes[a][:, t0:t1],
                         start=(a == 0),
                         stop=(a == PASSES - 1),
                     )
-            for h in range(2):
-                nc.scalar.activation(
-                    out=y[:, h * HALF : (h + 1) * HALF], in_=accs[h][:], func=IDENTITY, bias=bias[:, c : c + 1]
-                )
+            for i, (acc, (t0, t1)) in enumerate(zip(accs, PIECES)):
+                if c == 0 and i == 1:
+                    nc.vector.tensor_scalar(
+                        out=y[:, t0:t1], in0=acc[:], scalar1=bias[:, c : c + 1], scalar2=None, op0=ADD
+                    )
+                else:
+                    nc.scalar.activation(out=y[:, t0:t1], in_=acc[:], func=IDENTITY, bias=bias[:, c : c + 1])
             return y
 
-        def gather(y, products, c, d, v0, v1):
+        def gather(y, products, c, d):
             nc.vector.tensor_tensor(
-                out=products[:, d, v0:v1],
-                in0=y[:].indirect(lists[d][:, v0 // 16 : v1 // 16]),
-                in1=gates[c][:, d, v0:v1],
-                op=MULT,
+                out=products[:, d, :], in0=y[:].indirect(lists[d][:]), in1=gates[c][:, d, :], op=MULT
             )
 
-        def new_tiles():
-            products = work.tile([P, D, V], F32, name="products", align_bytes=64)
-            pairs = work.tile([P, 2, V], F32, name="pairs", align_bytes=64)
-            sums = work.tile([P, V], F32, name="sums", align_bytes=64)
-            return products, pairs, sums
+        def add(out_, a, b_):
+            nc.vector.tensor_tensor(out=out_, in0=a, in1=b_, op=ADD)
 
-        def add_pairs(tiles):
-            products, pairs, sums = tiles
-            nc.vector.tensor_tensor(out=pairs[:], in0=products[:, 0:2, :], in1=products[:, 2:4, :], op=ADD)
+        early = BLOCKS - 1
+        products = keep.tile([P, BLOCKS, D, V], F32, name="products", align_bytes=64)
+        pairs = keep.tile([P, BLOCKS, 2, V], F32, name="pairs", align_bytes=64)
+        sums = keep.tile([P, BLOCKS, V], F32, name="sums", align_bytes=64)
 
-        def add_rest(tiles, c):
-            products, pairs, sums = tiles
-            nc.vector.tensor_tensor(out=sums[:], in0=pairs[:, 0, :], in1=pairs[:, 1, :], op=ADD)
-            nc.sync.dma_start(out=out[c * P : (c + 1) * P, :], in_=sums[:])
+        def finish(c0, c1):
+            add(sums[:, c0:c1, :], pairs[:, c0:c1, 0, :], pairs[:, c0:c1, 1, :])
+            nc.sync.dma_start(
+                out=out[c0 * P : c1 * P, :].rearrange("(c p) v -> p c v", p=P), in_=sums[:, c0:c1, :]
+            )
 
         ys = [project(0)]
-        before = None
-        for c in range(BLOCKS - 1):
+        for c in range(early):
             ys.append(project(c + 1))
-            tiles = new_tiles()
-            gather(ys[c], tiles[0], c, 0, 0, V)
-            if before is not None:
-                add_pairs(before)
-            gather(ys[c], tiles[0], c, 1, 0, V)
-            if before is not None:
-                add_rest(before, c - 1)
-            gather(ys[c], tiles[0], c, 2, 0, V)
-            gather(ys[c], tiles[0], c, 3, 0, V)
-            before = tiles
+            for d in range(D):
+                gather(ys[c], products[:, c], c, d)
 
-        c = BLOCKS - 1
-        products, pairs, sums = new_tiles()
-        gather(ys[c], products, c, 0, 0, V)
-        add_pairs(before)
-        gather(ys[c], products, c, 1, 0, V)
-        add_rest(before, c - 1)
-        gather(ys[c], products, c, 2, 0, V)
-        nc.vector.tensor_tensor(out=pairs[:, 0, :], in0=products[:, 0, :], in1=products[:, 1, :], op=ADD)
-        gather(ys[c], products, c, 3, 0, V)
-        nc.vector.tensor_tensor(out=pairs[:, 1, :], in0=pairs[:, 0, :], in1=products[:, 2, :], op=ADD)
-        nc.vector.tensor_tensor(out=sums[:], in0=pairs[:, 1, :], in1=products[:, 3, :], op=ADD)
-        nc.sync.dma_start(out=out[c * P : N, :], in_=sums[:])
+        c = early
+        gather(ys[c], products[:, c], c, 0)
+        add(pairs[:, 0:early, :, :], products[:, 0:early, 0:2, :], products[:, 0:early, 2:4, :])
+        gather(ys[c], products[:, c], c, 1)
+        finish(0, early - 1)
+        gather(ys[c], products[:, c], c, 2)
+        add(pairs[:, c, 0, :], products[:, c, 0, :], products[:, c, 1, :])
+        gather(ys[c], products[:, c], c, 3)
+        add(pairs[:, c, 1, :], pairs[:, c, 0, :], products[:, c, 2, :])
+        finish(early - 1, early)
+        add(sums[:, c, :], pairs[:, c, 1, :], products[:, c, 3, :])
+        nc.sync.dma_start(out=out[c * P : N, :], in_=sums[:, c, :])

@@ -91,10 +91,10 @@ def tile_picked_agg_lin_bias_sub_l_kernel(tc, xT, w_words, w_scales, b, gate, po
         nc.sync.dma_start(out=lists[0][:], in_=pos1)
         load_gates(0, 0, 2)
         nc.sync.dma_start(out=lists[1][:], in_=pos2)
-        nc.sync.dma_start(out=lists[2][:], in_=pos3)
-        nc.sync.dma_start(out=lists[3][:], in_=pos4)
         load_gates(0, 2, D)
         load_weights(0, PASSES, P, 2 * P)
+        nc.sync.dma_start(out=lists[2][:], in_=pos3)
+        nc.sync.dma_start(out=lists[3][:], in_=pos4)
         load_gates(1, 0, D)
         load_weights(0, PASSES, 2 * P, N)
         load_gates(2, 0, D)

from contextlib import ExitStack

import concourse.mybir as mybir

K, T, D, V, N = 1024, 512, 4, 256, 512

F32 = mybir.dt.float32
BF16 = mybir.dt.bfloat16
U32 = mybir.dt.uint32
I32 = mybir.dt.int32
U16 = mybir.dt.uint16
U8 = mybir.dt.uint8
FP8X4 = mybir.dt.float8_e4m3fn_x4
ADD = mybir.AluOpType.add
MULT = mybir.AluOpType.mult
IDENTITY = mybir.ActivationFunctionType.Identity

FLOPS = 2 * K * T * N + 2 * D * N * V

P = 128
PACK = 4
K_PASS = P * PACK
PASSES = K // K_PASS
BLOCKS = N // P
PIECES = ((0, 256), (256, 384), (384, 512))
SPLIT = 336


def interleave(nc, grouped, raw, lanes, c0, c1, scalar):
    out = grouped[:, c0:c1, lanes]
    in_ = raw[:, lanes, c0:c1].rearrange("p j t -> p t j")
    if scalar:
        nc.scalar.copy(out=out, in_=in_)
    else:
        nc.vector.tensor_copy(out=out, in_=in_)


def tile_picked_agg_lin_bias_sub_l_kernel(tc, xT, w_words, w_scales, b, gate, pos1, pos2, pos3, pos4, out):
    nc = tc.nc
    with ExitStack() as ctx:
        keep = ctx.enter_context(tc.tile_pool(name="keep", bufs=1))
        ypool = ctx.enter_context(tc.tile_pool(name="ypool", bufs=3))
        psum = ctx.enter_context(tc.psum_pool(name="psum", bufs=1))

        lists = [keep.tile([P, V // 16], U16, name=f"list{d}") for d in range(D)]
        warm = keep.tile([P, 1], F32, name="warm")
        warm_out = keep.tile([P, 1], F32, name="warm_out")
        bias = keep.tile([P, BLOCKS], F32, name="bias")
        w_planes = keep.tile([P, N], U8, name="w_planes", align_bytes=256)
        w_codes = keep.tile([P, PASSES, N], U32, name="w_codes", align_bytes=256)
        raw = [keep.tile([P, PACK, T], F32, name=f"raw{a}", align_bytes=256) for a in range(PASSES)]
        grouped = [keep.tile([P, T, PACK], BF16, name=f"grouped{a}", align_bytes=256) for a in range(PASSES)]
        x_codes = [keep.tile([P, T], U32, name=f"x_codes{a}", align_bytes=256) for a in range(PASSES)]
        x_planes = [keep.tile([P, T], U8, name=f"x_planes{a}", align_bytes=256) for a in range(PASSES)]
        gates = [keep.tile([P, D, V], F32, name=f"gates{c}", align_bytes=256) for c in range(BLOCKS)]

        w_view = w_words.rearrange("a p m r -> p a (m r)")

        def load_weights(a0, a1, m0, m1):
            nc.sync.dma_start(
                out=w_codes[:, a0:a1, m0:m1].bitcast(I32),
                in_=w_view[:, a0:a1, PACK * m0 : PACK * m1].bitcast(I32),
            )

        def load_x(a, lanes):
            nc.sync.dma_start(
                out=raw[a][:, lanes, :],
                in_=xT[a * K_PASS : (a + 1) * K_PASS, :].rearrange("(p j) t -> p j t", j=PACK)[:, lanes, :],
            )

        def load_gates(c, d0, d1):
            nc.sync.dma_start(
                out=gates[c][:, d0:d1, :],
                in_=gate[d0:d1, c * P : (c + 1) * P, :].rearrange("d p v -> p d v"),
            )

        nc.vector.memset(w_planes[:].bitcast(I32), 0)
        nc.vector.memset(warm[:], 0.0)
        nc.scalar.activation(out=warm_out[:], in_=warm[:], func=IDENTITY)
        load_x(0, slice(0, PACK))
        for q in range(4):
            nc.sync.dma_start(
                out=w_planes[32 * q : 32 * q + 4 * PASSES, :].bitcast(I32),
                in_=w_scales[:, 4 * q : 4 * q + 4, :].bitcast(I32),
            )
        load_x(1, slice(0, 2))
        load_weights(0, 1, 0, P)
        load_x(1, slice(2, PACK))
        load_weights(1, 2, 0, P)
        nc.sync.dma_start(out=bias[:], in_=b.rearrange("(c p) o -> p (c o)", p=P))
        nc.sync.dma_start(out=lists[0][:], in_=pos1)
        load_gates(0, 0, 2)
        nc.sync.dma_start(out=lists[1][:], in_=pos2)
        load_gates(0, 2, D)
        load_weights(0, PASSES, P, 2 * P)
        nc.sync.dma_start(out=lists[2][:], in_=pos3)
        nc.sync.dma_start(out=lists[3][:], in_=pos4)
        load_gates(1, 0, D)
        load_weights(0, PASSES, 2 * P, N)
        load_gates(2, 0, D)
        load_gates(3, 0, D)


        def quantize(a, c0, c1):
            nc.vector.quantize_mx(
                out=x_codes[a][:, c0:c1].bitcast(FP8X4),
                scales=x_planes[a][:, c0:c1],
                in_=grouped[a][:, c0:c1, :].rearrange("p t j -> p (t j)"),
            )

        first = PIECES[0][1]
        everything = slice(0, PACK)
        interleave(nc, grouped[0], raw[0], everything, 0, first, False)
        interleave(nc, grouped[0], raw[0], everything, SPLIT, T, True)
        interleave(nc, grouped[0], raw[0], everything, first, SPLIT, False)
        quantize(0, 0, T)
        for lanes in (slice(0, 2), slice(2, PACK)):
            interleave(nc, grouped[1], raw[1], lanes, 0, first, False)
            interleave(nc, grouped[1], raw[1], lanes, SPLIT, T, True)
            interleave(nc, grouped[1], raw[1], lanes, first, SPLIT, False)
        for t0, t1 in PIECES:
            quantize(1, t0, t1)

        def project(c):
            y = ypool.tile([P, T], F32, name="y")
            cols = slice(c * P, (c + 1) * P)
            accs = [psum.tile([P, t1 - t0], F32, name=f"acc{t0}") for t0, t1 in PIECES]
            for a in range(PASSES):
                for acc, (t0, t1) in zip(accs, PIECES):
                    nc.tensor.matmul_mx(
                        out=acc[:],
                        lhsT=w_codes[:, a, cols].bitcast(FP8X4),
                        lhsT_scale=w_planes[4 * a : P, cols],
                        rhs=x_codes[a][:, t0:t1].bitcast(FP8X4),
                        rhs_scale=x_planes[a][:, t0:t1],
                        start=(a == 0),
                        stop=(a == PASSES - 1),
                    )
            for i, (acc, (t0, t1)) in enumerate(zip(accs, PIECES)):
                if c == 0 and i == 1:
                    nc.vector.tensor_scalar(
                        out=y[:, t0:t1], in0=acc[:], scalar1=bias[:, c : c + 1], scalar2=None, op0=ADD
                    )
                else:
                    nc.scalar.activation(out=y[:, t0:t1], in_=acc[:], func=IDENTITY, bias=bias[:, c : c + 1])
            return y

        def gather(y, products, c, d):
            nc.vector.tensor_tensor(
                out=products[:, d, :], in0=y[:].indirect(lists[d][:]), in1=gates[c][:, d, :], op=MULT
            )

        def add(out_, a, b_):
            nc.vector.tensor_tensor(out=out_, in0=a, in1=b_, op=ADD)

        early = BLOCKS - 1
        products = keep.tile([P, BLOCKS, D, V], F32, name="products", align_bytes=64)
        pairs = keep.tile([P, BLOCKS, 2, V], F32, name="pairs", align_bytes=64)
        sums = keep.tile([P, BLOCKS, V], F32, name="sums", align_bytes=64)

        def finish(c0, c1):
            add(sums[:, c0:c1, :], pairs[:, c0:c1, 0, :], pairs[:, c0:c1, 1, :])
            nc.sync.dma_start(
                out=out[c0 * P : c1 * P, :].rearrange("(c p) v -> p c v", p=P), in_=sums[:, c0:c1, :]
            )

        ys = [project(0)]
        for c in range(early):
            ys.append(project(c + 1))
            for d in range(D):
                gather(ys[c], products[:, c], c, d)

        c = early
        gather(ys[c], products[:, c], c, 0)
        add(pairs[:, 0:early, :, :], products[:, 0:early, 0:2, :], products[:, 0:early, 2:4, :])
        gather(ys[c], products[:, c], c, 1)
        finish(0, early - 1)
        gather(ys[c], products[:, c], c, 2)
        add(pairs[:, c, 0, :], products[:, c, 0, :], products[:, c, 1, :])
        gather(ys[c], products[:, c], c, 3)
        add(pairs[:, c, 1, :], pairs[:, c, 0, :], products[:, c, 2, :])
        finish(early - 1, early)
        add(sums[:, c, :], pairs[:, c, 1, :], products[:, c, 3, :])
        nc.sync.dma_start(out=out[c * P : N, :], in_=sums[:, c, :])
